import numpy as np
import ml_dtypes


def mxq(x, axis, fmt="e4m3"):
    dtype, down = {"e4m3": (ml_dtypes.float8_e4m3fn, 7), "e5m2": (ml_dtypes.float8_e5m2, 14)}[fmt]
    v = np.moveaxis(np.asarray(x, np.float32).astype(ml_dtypes.bfloat16).astype(np.float64), axis, -1)
    blocks = v.reshape(v.shape[:-1] + (-1, 32))
    amax = np.abs(blocks).max(-1, keepdims=True)
    byte = np.maximum(np.where(amax > 0, np.frexp(amax)[1] - 1 + 127, 0) - down, 1)
    scale = np.exp2(byte - 127.0)
    codes = (blocks / scale).astype(np.float32).astype(dtype).astype(np.float64)
    return np.moveaxis((codes * scale).reshape(v.shape), -1, axis)


WIDE = False


def mx_kscale(k):
    if not WIDE:
        return np.ones(k)
    levels = np.array([10, -10, 5, -5, 0])
    if k % 512:
        return np.exp2(np.random.permutation(np.resize(levels, k // 32))).repeat(32)
    a = np.empty((k // 512, 16))
    for p in range(k // 512):
        a[p, :8] = np.random.permutation(np.resize(levels, 8))
        for g in range(8):
            far = levels[np.abs(levels - a[p, g]) >= 10]
            a[p, g + 8] = far[np.random.randint(len(far))]
    return np.exp2(a.ravel()).repeat(32)


def f64(x):
    return np.asarray(x).astype(np.float64)


def striped(idx):
    return np.tile(idx.reshape(-1, 16).T, (8, 1)).astype(np.uint16)


def unstriped(offs):
    return offs[:16].T.reshape(-1).astype(np.int64)


def pack_weight(w):
    k, n = w.shape
    w = f64(np.asarray(w, np.float32).astype(ml_dtypes.bfloat16)).reshape(k // 32, 32, n)
    amax = np.abs(w).max(1)
    byte = np.clip(np.where(amax > 0, np.frexp(amax)[1] - 1 + 127 - 7, 1), 1, 254)
    scaled = (w * np.exp2(127.0 - byte)[:, None, :]).reshape(k, n).astype(np.float32)
    words = np.ascontiguousarray(scaled.reshape(k // 512, 128, 4, n).transpose(0, 1, 3, 2)).astype(ml_dtypes.float8_e4m3fn).view(np.uint8)
    return words, np.ascontiguousarray(byte.astype(np.uint8).reshape(k // 512, 16, n))


def unpack_weight(words, scales):
    g, p, n, _ = words.shape
    vals = np.ascontiguousarray(words).view(ml_dtypes.float8_e4m3fn).astype(np.float64) * np.repeat(np.exp2(scales.astype(np.float64) - 127.0), 8, axis=1)[..., None]
    return vals.transpose(0, 1, 3, 2).reshape(g * 512, n)


def relu(v):
    return np.maximum(v, 0.0)


K, T, S, V, D, W = 512, 1024, 512, 512, 8, 2048


def setup_inputs():
    n = np.random.standard_normal
    s = mx_kscale(K)[:, None]
    packed_xT = pack_weight(n((K, T)) * s)
    packed_eT = pack_weight(n((K, W)) * s)
    return {
        "x_words": packed_xT[0],
        "x_scales": packed_xT[1],
        "e_words": packed_eT[0],
        "e_scales": packed_eT[1],
        "wq": (n((K, V)) / np.sqrt(K) / s).astype(np.float32),
        "wh": (n((K, V)) / np.sqrt(K) / s).astype(np.float32),
        "wo": (n((K, V)) / np.sqrt(K) / s).astype(np.float32),
        "offs": striped(np.random.permutation(T)[:S]),
        "obs": striped(np.random.permutation(W)[:S]),
    }


def reference(x_words, x_scales, e_words, e_scales, wq, wh, wo, offs, obs):
    xq = unpack_weight(x_words, x_scales)[:, unstriped(offs)]
    whq = mxq(f64(wh), 0, "e4m3")
    e_obs = unpack_weight(e_words, e_scales)[:, unstriped(obs)]
    woq = mxq(f64(wo), 0, "e4m3")
    z = xq.T @ whq + e_obs.T @ woq
    eq = np.exp(z)
    sq = eq.reshape(len(eq), -1, D).sum(axis=2)
    q1 = 0.99 * (eq / np.repeat(sq, D, axis=1)) + 0.00125
    wqq = mxq(f64(wq), 0, "e4m3")
    y = xq.T @ wqq
    ep = np.exp(y)
    sp = ep.reshape(len(ep), -1, D).sum(axis=2)
    p1 = 0.99 * (ep / np.repeat(sp, D, axis=1)) + 0.00125
    kl = q1 * (np.log(q1) - np.log(p1))
    return relu(kl.reshape(len(kl), -1, D).sum(axis=2) - 0.3)

@@ -1,0 +1,286 @@
+from contextlib import ExitStack
+
+import concourse.mybir as mybir
+from concourse.masks import make_identity
+
+F32 = mybir.dt.float32
+BF16 = mybir.dt.bfloat16
+I32 = mybir.dt.int32
+U32 = mybir.dt.uint32
+U16 = mybir.dt.uint16
+U8 = mybir.dt.uint8
+FP8X4 = mybir.dt.float8_e4m3fn_x4
+ALU = mybir.AluOpType
+ACT = mybir.ActivationFunctionType
+AXIS = mybir.AxisListType
+
+P = 128
+S = 512
+V = 512
+D = 8
+G = V // D
+PACK = 4
+TILES = S // P
+PAIRS = TILES // 2
+HALF = D // 2
+KEEP = 0.99
+FLOOR = 0.00125
+FREE = 0.3
+FLOPS = 3 * 2 * 512 * S * V
+
+
+def tile_picked_ydream_free_p_kernel(
+    tc, x_words, x_scales, e_words, e_scales, wq, wh, wo, offs, obs, out
+):
+    nc = tc.nc
+    with ExitStack() as ctx:
+        keep = ctx.enter_context(tc.tile_pool(name="keep", bufs=1))
+        psum = ctx.enter_context(tc.psum_pool(name="psum", bufs=1))
+
+        def bank(index, name):
+            return psum.tile([P, 512], F32, name=name, tag="bank%d" % index)
+
+        def load_list(source, name):
+            tile = keep.tile([P, S // 16], U16, name=name)
+            nc.sync.dma_start(tile[:], source)
+            return tile
+
+        def load_words(source, name):
+            tile = keep.tile([P, source.shape[2]], I32, name=name, align_bytes=64)
+            nc.sync.dma_start(tile[:], source[0].rearrange("p c r -> p (c r)").bitcast(I32))
+            return tile
+
+        def load_scales(source, name):
+            tile = keep.tile([P, source.shape[2]], U8, name=name, align_bytes=64)
+            nc.gpsimd.memset(tile[:].bitcast(I32), 0)
+            for q in range(4):
+                nc.sync.dma_start(tile[32 * q : 32 * q + 4, :].bitcast(I32), source[0, 4 * q : 4 * q + 4, :].bitcast(I32))
+            return tile
+
+        def load_weight(source, cols, name):
+            tile = keep.tile([P, PACK, cols.stop - cols.start], F32, name=name, align_bytes=64)
+            nc.sync.dma_start(tile[:], source.rearrange("(p j) c -> p j c", j=PACK)[:, :, cols])
+            return tile
+
+        def cast_views(raw, name):
+            grouped = keep.tile([P, raw.shape[2], PACK], BF16, name=name, align_bytes=64)
+            dst = grouped[:].rearrange("p (c i) j -> p c j i", i=4)
+            src = raw[:].rearrange("p j (c i) -> p c j i", i=4)
+            return grouped, dst, src
+
+        def quantise(grouped, codes, scales):
+            nc.vector.quantize_mx(out=codes.bitcast(FP8X4), scales=scales, in_=grouped[:].rearrange("p c j -> p (c j)"))
+
+        def mx_tiles(name):
+            codes = keep.tile([P, 512], U32, name=name + "_codes", align_bytes=64)
+            scales = keep.tile([P, 512], U8, name=name + "_scales", align_bytes=64)
+            return codes, scales
+
+        halves = [slice(0, V // 2), slice(V // 2, V)]
+        offs_sb = load_list(offs, "offs_sb")
+        x_table = load_words(x_words, "x_table")
+        x_plane = load_scales(x_scales, "x_plane")
+        wq_raw = load_weight(wq, slice(0, V), "wq_raw")
+        obs_sb = load_list(obs, "obs_sb")
+        e_plane = load_scales(e_scales, "e_plane")
+        wh_raw = load_weight(wh, slice(0, V), "wh_raw")
+        wo_raw = load_weight(wo, slice(0, V), "wo_raw")
+        e_table = load_words(e_words, "e_table")
+
+        x_codes, x_bytes = mx_tiles("x")
+        e_codes, e_bytes = mx_tiles("e")
+        wq_codes, wq_bytes = mx_tiles("wq")
+        wh_codes, wh_bytes = mx_tiles("wh")
+        wo_codes, wo_bytes = mx_tiles("wo")
+
+        def cast_on_gpsimd(raw, name):
+            grouped = keep.tile([P, raw.shape[2], PACK], BF16, name=name, tag=name, align_bytes=64)
+            nc.gpsimd.tensor_scalar(grouped[:], raw[:].rearrange("p j c -> p c j"), 1.0, 0.0, ALU.mult, ALU.add)
+            return grouped
+
+        def cast_on_scalar(raw, name):
+            grouped, dst, src = cast_views(raw, name)
+            nc.scalar.copy(dst, src)
+            return grouped
+
+        def gather_words(codes, table, offsets, h):
+            nc.vector.tensor_copy(
+                codes[:, h * 256 : (h + 1) * 256], table[:].bitcast(U32).indirect(offsets[:, h * 16 : (h + 1) * 16])
+            )
+
+        ident = keep.tile([P, P], F32, name="ident")
+        make_identity(nc, ident[:])
+        wq_low = cast_on_gpsimd(wq_raw[:, :, halves[0]], "wq_low")
+        wq_high = cast_on_scalar(wq_raw[:, :, halves[1]], "wq_high")
+        wh_grouped = cast_on_scalar(wh_raw, "wh_grouped")
+        wo_grouped = cast_on_gpsimd(wo_raw, "wo_grouped")
+
+        nc.vector.tensor_copy(x_codes[:], x_table[:].bitcast(U32).indirect(offs_sb[:]))
+        nc.vector.tensor_copy(x_bytes[:], x_plane[:].indirect(offs_sb[:]))
+        nc.vector.tensor_copy(e_bytes[:], e_plane[:].indirect(obs_sb[:]))
+        quantise(wq_low, wq_codes[:, halves[0]], wq_bytes[:, halves[0]])
+        quantise(wq_high, wq_codes[:, halves[1]], wq_bytes[:, halves[1]])
+
+        def product(logits, tile, codes, scales, w_codes, w_scales, start, stop):
+            rows = slice(tile * P, (tile + 1) * P)
+            nc.tensor.matmul_mx(
+                out=logits[:], lhsT=codes[:, rows].bitcast(FP8X4), lhsT_scale=scales[:, rows],
+                rhs=w_codes[:].bitcast(FP8X4), rhs_scale=w_scales[:], start=start, stop=stop,
+            )
+
+        def add_transposed(dst, src, start, stop):
+            nc.tensor.matmul(dst, src, ident[:], start=start, stop=stop, is_transpose=True)
+
+        def shift(logits, name):
+            peaks = keep.tile([P, TILES, G], F32, name=name + "_peaks")
+            shifted = keep.tile([P, TILES, V], F32, name=name + "_shifted", tag=name + "_stage")
+
+            def peak(tile):
+                nc.vector.tensor_reduce(peaks[:, tile, :], logits[tile][:].rearrange("p (g d) -> p g d", d=D), AXIS.X, ALU.max)
+
+            peak(0)
+            for tile in range(TILES):
+                if tile + 1 < TILES:
+                    peak(tile + 1)
+                by_class = shifted[:, tile, :].rearrange("p (d g) -> p d g", d=D)
+                nc.vector.tensor_tensor(
+                    by_class, logits[tile][:].rearrange("p (g d) -> p d g", d=D),
+                    peaks[:, tile, :].unsqueeze(1).to_broadcast([P, D, G]), ALU.subtract,
+                )
+            return shifted
+
+        def exponentials(shifted, pair, name, tag):
+            powers = keep.tile([P, D, 2, G], F32, name=name, tag=tag, align_bytes=64)
+            for t in range(2):
+                nc.scalar.activation(powers[:, :, t, :], shifted[:, 2 * pair + t, :].rearrange("p (d g) -> p d g", d=D), ACT.Exp)
+            return powers
+
+        def mixtures(powers, sums, banks, name, scale_on_vector, copy_on_vector, floors_t, floors):
+            def block(d):
+                return powers[:, d, :, :].rearrange("p t g -> p (t g)")
+
+            def spread(a, mixed):
+                for j in range(HALF):
+                    add_transposed(mixed[:, j * P : (j + 1) * P], block(a * HALF + j), j == 0, False)
+
+            def add_floors(mixed):
+                for j in range(HALF):
+                    add_transposed(mixed[:, j * P : (j + 1) * P], floors, False, j == HALF - 1)
+
+            for d in range(D):
+                add_transposed(sums[:, 0:P], block(d), d == 0, d == D - 1)
+            first = bank(banks[0], name + "_mixed0")
+            spread(0, first)
+            if scale_on_vector:
+                nc.vector.tensor_scalar(floors_t, sums[:, 0:P], FLOOR / KEEP, None, ALU.mult)
+            else:
+                nc.scalar.activation(floors_t, sums[:, 0:P], ACT.Copy, scale=FLOOR / KEEP)
+            nc.tensor.transpose(sums[:, P : 2 * P], floors_t, ident[:])
+            if copy_on_vector:
+                nc.vector.tensor_copy(floors, sums[:, P : 2 * P])
+            else:
+                nc.scalar.copy(floors, sums[:, P : 2 * P])
+            add_floors(first)
+            second = bank(banks[1], name + "_mixed1")
+            spread(1, second)
+            add_floors(second)
+            return [first, second]
+
+        floors_t = keep.tile([P, 2, PAIRS, P], F32, name="floors_t")
+        floors = keep.tile([P, 2, PAIRS, P], F32, name="floors")
+
+        y = [bank(tile, "y%d" % tile) for tile in range(TILES)]
+        for tile in range(TILES):
+            product(y[tile], tile, x_codes, x_bytes, wq_codes, wq_bytes, True, True)
+        p_shifted = shift(y, "p")
+        p_powers = [exponentials(p_shifted, 0, "p_powers0", "p_powers0")]
+
+        z = [bank(TILES + tile, "z%d" % tile) for tile in range(TILES - 1)]
+        quantise(wh_grouped, wh_codes[:], wh_bytes[:])
+        for tile in range(TILES - 1):
+            product(z[tile], tile, x_codes, x_bytes, wh_codes, wh_bytes, True, False)
+        gather_words(e_codes, e_table, obs_sb, 0)
+        quantise(wo_grouped, wo_codes[:], wo_bytes[:])
+        gather_words(e_codes, e_table, obs_sb, 1)
+        for tile in range(TILES - 1):
+            product(z[tile], tile, e_codes, e_bytes, wo_codes, wo_bytes, False, True)
+
+        p_powers.append(exponentials(p_shifted, 1, "p_powers1", "wo_grouped"))
+        p_sums = bank(2 * TILES - 1, "p0_sums")
+        p_mixed = mixtures(p_powers[0], p_sums, [0, 1], "p0", False, False, floors_t[:, 0, 0, :], floors[:, 0, 0, :])
+        z.append(bank(2 * TILES - 1, "z3"))
+        product(z[3], 3, x_codes, x_bytes, wh_codes, wh_bytes, True, False)
+        product(z[3], 3, e_codes, e_bytes, wo_codes, wo_bytes, False, True)
+        late = p_powers[1][:].rearrange("p d t g -> p d (t g)")
+        fold = keep.tile([P, HALF, P], F32, name="fold")
+        fold2 = keep.tile([P, 2, P], F32, name="fold2")
+        fold3 = keep.tile([P, P], F32, name="fold3")
+        late_mixed = keep.tile([P, D, P], F32, name="late_mixed")
+        nc.gpsimd.tensor_tensor(fold[:], late[:, :HALF, :], late[:, HALF:, :], ALU.add)
+        nc.gpsimd.tensor_tensor(fold2[:], fold[:, :2, :], fold[:, 2:, :], ALU.add)
+        nc.gpsimd.tensor_tensor(fold3[:], fold2[:, 0, :], fold2[:, 1, :], ALU.add)
+        nc.gpsimd.tensor_scalar(floors[:, 0, 1, :], fold3[:], FLOOR / KEEP, 0.0, ALU.mult, ALU.add)
+        for a in range(2):
+            nc.gpsimd.tensor_tensor(
+                late_mixed[:, a * HALF : (a + 1) * HALF, :], late[:, a * HALF : (a + 1) * HALF, :],
+                floors[:, 0, 1, :].unsqueeze(1).to_broadcast([P, HALF, P]), ALU.add,
+            )
+        p_sums = bank(3, "p1_sums")
+        nc.tensor.transpose(p_sums[:, 0:P], floors[:, 0, 1, :], ident[:])
+        nc.scalar.copy(floors_t[:, 0, 1, :], p_sums[:, 0:P])
+
+        q_shifted = shift(z, "q")
+        q_powers = [exponentials(q_shifted, pair, "q_powers%d" % pair, "q_powers%d" % pair) for pair in range(PAIRS)]
+        q_mixed = []
+        inverse = keep.tile([P, PAIRS, P], F32, name="inverse")
+        for pair in range(PAIRS):
+            q_sums = bank(TILES + 2 * pair, "q%d_sums" % pair)
+            q_mixed.extend(
+                mixtures(
+                    q_powers[pair], q_sums, [TILES + 2 * pair + 1, TILES + 2 * pair], "q%d" % pair, pair == PAIRS - 1, True,
+                    floors_t[:, 1, pair, :], floors[:, 1, pair, :],
+                )
+            )
+
+        for a in range(2):
+            mixed = bank(2 + a, "p1_mixed%d" % a)
+            for j in range(HALF):
+                nc.tensor.transpose(mixed[:, j * P : (j + 1) * P], late_mixed[:, a * HALF + j, :], ident[:])
+            p_mixed.append(mixed)
+
+        logs = keep.tile([P, 2 * TILES + 1, V], F32, name="logs", tag="q_stage")
+        log_floors = logs[:, 2 * TILES, :]
+        cross = [keep.tile([P, V], F32, name="cross%d" % a) for a in range(TILES)]
+        own = [keep.tile([P, V], F32, name="own%d" % a) for a in range(TILES)]
+        margin = keep.tile([P, PAIRS * P], F32, name="margin")
+        shortfall = keep.tile([P, PAIRS * P], F32, name="shortfall")
+        allowance = keep.tile([P, PAIRS, P], F32, name="allowance")
+        nc.vector.reciprocal(inverse[:, 0, :], floors[:, 1, 0, :])
+        for a in range(TILES):
+            nc.scalar.activation(logs[:, 2 * a, :], p_mixed[a][:], ACT.Ln)
+            nc.scalar.activation(logs[:, 2 * a + 1, :], q_mixed[a][:], ACT.Ln)
+            nc.vector.scalar_tensor_tensor(cross[a][:], q_mixed[a][:], -FLOOR, logs[:, 2 * a, :], ALU.mult, ALU.mult)
+            nc.vector.scalar_tensor_tensor(own[a][:], q_mixed[a][:], FLOOR, logs[:, 2 * a + 1, :], ALU.mult, ALU.mult)
+            if a == 1:
+                nc.scalar.activation(log_floors, floors_t[:].rearrange("p s a t -> p (s a t)"), ACT.Ln)
+                nc.gpsimd.tensor_tensor(margin[:], log_floors[:, : PAIRS * P], log_floors[:, PAIRS * P :], ALU.subtract)
+                nc.gpsimd.tensor_scalar(shortfall[:], margin[:], 1.0, -FREE, ALU.mult, ALU.add)
+                nc.gpsimd.tensor_tensor(
+                    allowance[:].rearrange("p a t -> p (a t)"), shortfall[:], floors_t[:, 1, :, :].rearrange("p a t -> p (a t)"), ALU.mult
+                )
+
+        nc.vector.reciprocal(inverse[:, 1, :], floors[:, 1, 1, :])
+        result = keep.tile([P, TILES, G], F32, name="result")
+        for pair in range(PAIRS):
+            total = bank(2 * pair, "total%d" % pair)
+            terms = [term[a][:, j * P : (j + 1) * P] for a in (2 * pair, 2 * pair + 1) for term in (cross, own) for j in range(HALF)]
+            terms = terms[:-HALF] + [allowance[:, pair, :]] + terms[-HALF:] if pair else terms + [allowance[:, pair, :]]
+            for n, term in enumerate(terms):
+                add_transposed(total[:, 0:P], term, n == 0, n == len(terms) - 1)
+            nc.vector.scalar_tensor_tensor(
+                result[:, 2 * pair : 2 * pair + 2, :].rearrange("p t g -> p (t g)"), total[:, 0:P], 0.0, inverse[:, pair, :],
+                ALU.max, ALU.mult,
+            )
+            nc.sync.dma_start(
+                out[2 * pair * P : (2 * pair + 2) * P, :].rearrange("(t p) g -> p t g", p=P), result[:, 2 * pair : 2 * pair + 2, :]
+            )

@@ -50,15 +50,15 @@ def tile_picked_ydream_free_p_kernel(
             nc.sync.dma_start(tile[:], source[0].rearrange("p c r -> p (c r)").bitcast(I32))
             return tile
 
-        def load_scales(source, name):
+        def load_scales(queue, source, name):
             tile = keep.tile([P, source.shape[2]], U8, name=name, align_bytes=64)
             nc.gpsimd.memset(tile[:].bitcast(I32), 0)
             for q in range(4):
-                nc.sync.dma_start(tile[32 * q : 32 * q + 4, :].bitcast(I32), source[0, 4 * q : 4 * q + 4, :].bitcast(I32))
+                queue.dma_start(tile[32 * q : 32 * q + 4, :].bitcast(I32), source[0, 4 * q : 4 * q + 4, :].bitcast(I32))
             return tile
 
         def load_weight(source, cols, name):
-            tile = keep.tile([P, PACK, cols.stop - cols.start], F32, name=name, align_bytes=64)
+            tile = keep.tile([P, PACK, cols.stop - cols.start], F32, name=name, tag=name, align_bytes=64)
             nc.sync.dma_start(tile[:], source.rearrange("(p j) c -> p j c", j=PACK)[:, :, cols])
             return tile
 
@@ -79,10 +79,10 @@ def tile_picked_ydream_free_p_kernel(
         halves = [slice(0, V // 2), slice(V // 2, V)]
         offs_sb = load_list(offs, "offs_sb")
         x_table = load_words(x_words, "x_table")
-        x_plane = load_scales(x_scales, "x_plane")
-        wq_raw = load_weight(wq, slice(0, V), "wq_raw")
+        x_plane = load_scales(nc.scalar, x_scales, "x_plane")
         obs_sb = load_list(obs, "obs_sb")
-        e_plane = load_scales(e_scales, "e_plane")
+        wq_raw = load_weight(wq, slice(0, V), "wq_raw")
+        e_plane = load_scales(nc.sync, e_scales, "e_plane")
         wh_raw = load_weight(wh, slice(0, V), "wh_raw")
         wo_raw = load_weight(wo, slice(0, V), "wo_raw")
         e_table = load_words(e_words, "e_table")
@@ -110,16 +110,15 @@ def tile_picked_ydream_free_p_kernel(
 
         ident = keep.tile([P, P], F32, name="ident")
         make_identity(nc, ident[:])
-        wq_low = cast_on_gpsimd(wq_raw[:, :, halves[0]], "wq_low")
         wq_high = cast_on_scalar(wq_raw[:, :, halves[1]], "wq_high")
-        wh_grouped = cast_on_scalar(wh_raw, "wh_grouped")
-        wo_grouped = cast_on_gpsimd(wo_raw, "wo_grouped")
 
         nc.vector.tensor_copy(x_codes[:], x_table[:].bitcast(U32).indirect(offs_sb[:]))
         nc.vector.tensor_copy(x_bytes[:], x_plane[:].indirect(offs_sb[:]))
-        nc.vector.tensor_copy(e_bytes[:], e_plane[:].indirect(obs_sb[:]))
+        wq_low, dst, src = cast_views(wq_raw[:, :, halves[0]], "wq_low")
+        nc.vector.tensor_copy(dst, src)
         quantise(wq_low, wq_codes[:, halves[0]], wq_bytes[:, halves[0]])
         quantise(wq_high, wq_codes[:, halves[1]], wq_bytes[:, halves[1]])
+        nc.vector.tensor_copy(e_bytes[:], e_plane[:].indirect(obs_sb[:]))
 
         def product(logits, tile, codes, scales, w_codes, w_scales, start, stop):
             rows = slice(tile * P, (tile + 1) * P)
@@ -131,29 +130,20 @@ def tile_picked_ydream_free_p_kernel(
         def add_transposed(dst, src, start, stop):
             nc.tensor.matmul(dst, src, ident[:], start=start, stop=stop, is_transpose=True)
 
-        def shift(logits, name):
-            peaks = keep.tile([P, TILES, G], F32, name=name + "_peaks")
-            shifted = keep.tile([P, TILES, V], F32, name=name + "_shifted", tag=name + "_stage")
+        def by_class(logits):
+            return logits[:].rearrange("p (g d) -> p d g", d=D)
 
-            def peak(tile):
-                nc.vector.tensor_reduce(peaks[:, tile, :], logits[tile][:].rearrange("p (g d) -> p g d", d=D), AXIS.X, ALU.max)
+        def peak(logits, name):
+            peaks = keep.tile([P, G], F32, name=name)
+            nc.vector.tensor_reduce(peaks[:], logits[:].rearrange("p (g d) -> p g d", d=D), AXIS.X, ALU.max)
+            return peaks
 
-            peak(0)
-            for tile in range(TILES):
-                if tile + 1 < TILES:
-                    peak(tile + 1)
-                by_class = shifted[:, tile, :].rearrange("p (d g) -> p d g", d=D)
-                nc.vector.tensor_tensor(
-                    by_class, logits[tile][:].rearrange("p (g d) -> p d g", d=D),
-                    peaks[:, tile, :].unsqueeze(1).to_broadcast([P, D, G]), ALU.subtract,
-                )
-            return shifted
+        def shift(engine, shifted, source, peaks):
+            engine.tensor_tensor(shifted, source, peaks[:].unsqueeze(1).to_broadcast([P, D, G]), ALU.subtract)
 
-        def exponentials(shifted, pair, name, tag):
-            powers = keep.tile([P, D, 2, G], F32, name=name, tag=tag, align_bytes=64)
+        def exponentials(powers, shifted):
             for t in range(2):
-                nc.scalar.activation(powers[:, :, t, :], shifted[:, 2 * pair + t, :].rearrange("p (d g) -> p d g", d=D), ACT.Exp)
-            return powers
+                nc.scalar.activation(powers[:, :, t, :], shifted[t], ACT.Exp)
 
         def mixtures(powers, sums, banks, name, scale_on_vector, copy_on_vector, floors_t, floors):
             def block(d):
@@ -186,32 +176,46 @@ def tile_picked_ydream_free_p_kernel(
             add_floors(second)
             return [first, second]
 
-        floors_t = keep.tile([P, 2, PAIRS, P], F32, name="floors_t")
         floors = keep.tile([P, 2, PAIRS, P], F32, name="floors")
+        p_floors_t = keep.tile([P, P], F32, name="p_floors_t", tag="p_floors_t", align_bytes=64)
 
         y = [bank(tile, "y%d" % tile) for tile in range(TILES)]
         for tile in range(TILES):
             product(y[tile], tile, x_codes, x_bytes, wq_codes, wq_bytes, True, True)
-        p_shifted = shift(y, "p")
-        p_powers = [exponentials(p_shifted, 0, "p_powers0", "p_powers0")]
+        z = [bank(TILES + tile, "z%d" % tile) for tile in range(TILES)]
 
-        z = [bank(TILES + tile, "z%d" % tile) for tile in range(TILES - 1)]
+        wh_grouped = cast_on_scalar(wh_raw, "wh_grouped")
+        wo_grouped = cast_on_gpsimd(wo_raw, "wo_grouped")
+        after_wh = keep.tile([P, 2, D, 2, G], F32, name="after_wh", tag="wh_raw", align_bytes=64)
+        after_wo = keep.tile([P, 2, D, G], F32, name="after_wo", tag="wo_raw", align_bytes=64)
+        p_powers = [after_wh[:, 0], keep.tile([P, D, 2, G], F32, name="p_powers1")[:]]
+        plain = after_wh[:, 1].rearrange("p d t g -> p (d t g)").rearrange("p (t d g) -> p t d g", t=2, d=D)
+        p_shifted = [keep.tile([P, D, G], F32, name="p_shifted0")[:], None, after_wo[:, 0], after_wo[:, 1]]
+        p_peaks = [peak(y[0], "p_peaks0"), peak(y[1], "p_peaks1")]
+        shift(nc.vector, p_shifted[0], by_class(y[0]), p_peaks[0])
+        p_peaks.append(peak(y[2], "p_peaks2"))
         quantise(wh_grouped, wh_codes[:], wh_bytes[:])
-        for tile in range(TILES - 1):
+        for tile in range(TILES):
             product(z[tile], tile, x_codes, x_bytes, wh_codes, wh_bytes, True, False)
+        p_peaks.append(peak(y[3], "p_peaks3"))
+        for t in range(2):
+            nc.scalar.copy(plain[:, t], by_class(y[2 + t]))
+            shift(nc.gpsimd, p_shifted[2 + t], plain[:, t], p_peaks[2 + t])
         gather_words(e_codes, e_table, obs_sb, 0)
         quantise(wo_grouped, wo_codes[:], wo_bytes[:])
         gather_words(e_codes, e_table, obs_sb, 1)
-        for tile in range(TILES - 1):
+        for tile in range(TILES):
             product(z[tile], tile, e_codes, e_bytes, wo_codes, wo_bytes, False, True)
+        p_shifted[1] = keep.tile([P, D, G], F32, name="p_shifted1", tag="wo_grouped", align_bytes=64)[:]
+        shift(nc.vector, p_shifted[1], by_class(y[1]), p_peaks[1])
+        exponentials(p_powers[1], p_shifted[2:])
+        exponentials(p_powers[0], p_shifted[:2])
 
-        p_powers.append(exponentials(p_shifted, 1, "p_powers1", "wo_grouped"))
-        p_sums = bank(2 * TILES - 1, "p0_sums")
-        p_mixed = mixtures(p_powers[0], p_sums, [0, 1], "p0", False, False, floors_t[:, 0, 0, :], floors[:, 0, 0, :])
-        z.append(bank(2 * TILES - 1, "z3"))
-        product(z[3], 3, x_codes, x_bytes, wh_codes, wh_bytes, True, False)
-        product(z[3], 3, e_codes, e_bytes, wo_codes, wo_bytes, False, True)
-        late = p_powers[1][:].rearrange("p d t g -> p d (t g)")
+        p_sums = bank(TILES - 1, "p0_sums")
+        p_floors = keep.tile([P, P], F32, name="p_floors", tag="p_floors", align_bytes=64)
+        p_mixed = mixtures(p_powers[0], p_sums, [0, 1], "p0", False, False, p_floors_t[:], floors[:, 0, 0, :])
+
+        late = p_powers[1].rearrange("p d t g -> p d (t g)")
         fold = keep.tile([P, HALF, P], F32, name="fold")
         fold2 = keep.tile([P, 2, P], F32, name="fold2")
         fold3 = keep.tile([P, P], F32, name="fold3")
@@ -225,60 +229,77 @@ def tile_picked_ydream_free_p_kernel(
                 late_mixed[:, a * HALF : (a + 1) * HALF, :], late[:, a * HALF : (a + 1) * HALF, :],
                 floors[:, 0, 1, :].unsqueeze(1).to_broadcast([P, HALF, P]), ALU.add,
             )
-        p_sums = bank(3, "p1_sums")
-        nc.tensor.transpose(p_sums[:, 0:P], floors[:, 0, 1, :], ident[:])
-        nc.scalar.copy(floors_t[:, 0, 1, :], p_sums[:, 0:P])
-
-        q_shifted = shift(z, "q")
-        q_powers = [exponentials(q_shifted, pair, "q_powers%d" % pair, "q_powers%d" % pair) for pair in range(PAIRS)]
-        q_mixed = []
-        inverse = keep.tile([P, PAIRS, P], F32, name="inverse")
+        q_shifted = [keep.tile([P, D, G], F32, name="q_shifted%d" % t, tag="q_stage%d" % t)[:] for t in range(TILES)]
+        q_powers = [keep.tile([P, D, 2, G], F32, name="q_powers%d" % pair)[:] for pair in range(PAIRS)]
+        q_peaks = [peak(z[0], "q_peaks0")]
+        for tile in range(TILES):
+            if tile + 1 < TILES:
+                q_peaks.append(peak(z[tile + 1], "q_peaks%d" % (tile + 1)))
+            shift(nc.vector, q_shifted[tile], by_class(z[tile]), q_peaks[tile])
         for pair in range(PAIRS):
-            q_sums = bank(TILES + 2 * pair, "q%d_sums" % pair)
-            q_mixed.extend(
-                mixtures(
-                    q_powers[pair], q_sums, [TILES + 2 * pair + 1, TILES + 2 * pair], "q%d" % pair, pair == PAIRS - 1, True,
-                    floors_t[:, 1, pair, :], floors[:, 1, pair, :],
-                )
-            )
-
-        for a in range(2):
-            mixed = bank(2 + a, "p1_mixed%d" % a)
+            exponentials(q_powers[pair], q_shifted[2 * pair : 2 * pair + 2])
+        q_mixed = []
+        for pair in range(PAIRS):
+            powers = q_powers[pair]
+            halved = keep.tile([P, HALF, 2, G], F32, name="halved%d" % pair)
+            summed = keep.tile([P, P], F32, name="summed%d" % pair)
+            for tiles in [slice(0, 2)] if pair == 0 else [slice(0, 1), slice(1, 2)]:
+                nc.vector.tensor_tensor(halved[:, :, tiles, :], powers[:, :HALF, tiles, :], powers[:, HALF:, tiles, :], ALU.add)
+            nc.vector.tensor_reduce(summed[:], halved[:].rearrange("p d t g -> p (t g) d"), AXIS.X, ALU.add)
+            nc.vector.tensor_scalar(floors[:, 1, pair, :], summed[:], FLOOR / KEEP, None, ALU.mult)
+            for a in range(2):
+                mixed = bank(TILES + 2 * pair + a, "q%d_mixed%d" % (pair, a))
+                for j in range(HALF):
+                    add_transposed(mixed[:, j * P : (j + 1) * P], powers[:, a * HALF + j, :, :].rearrange("p t g -> p (t g)"), j == 0, False)
+                q_mixed.append(mixed)
+        for a in range(TILES):
             for j in range(HALF):
-                nc.tensor.transpose(mixed[:, j * P : (j + 1) * P], late_mixed[:, a * HALF + j, :], ident[:])
-            p_mixed.append(mixed)
-
-        logs = keep.tile([P, 2 * TILES + 1, V], F32, name="logs", tag="q_stage")
+                add_transposed(q_mixed[a][:, j * P : (j + 1) * P], floors[:, 1, a // 2, :], False, j == HALF - 1)
+            if a == 1:
+                for b in range(2):
+                    mixed = bank(2 + b, "p1_mixed%d" % b)
+                    for j in range(HALF):
+                        nc.tensor.transpose(mixed[:, j * P : (j + 1) * P], late_mixed[:, b * HALF + j, :], ident[:])
+                    p_mixed.append(mixed)
+        logs = keep.tile([P, 2 * TILES + 1, V], F32, name="logs", tag="q_stage%d" % (TILES - 1))
         log_floors = logs[:, 2 * TILES, :]
-        cross = [keep.tile([P, V], F32, name="cross%d" % a) for a in range(TILES)]
+        p_logs = [logs[:, 2 * a, :] for a in range(TILES)]
+        q_logs = [logs[:, 2 * a + 1, :] for a in range(TILES)]
+        gaps = [keep.tile([P, V], F32, name="gap%d" % a, tag="gap%d" % a) for a in range(TILES)]
         own = [keep.tile([P, V], F32, name="own%d" % a) for a in range(TILES)]
         margin = keep.tile([P, PAIRS * P], F32, name="margin")
-        shortfall = keep.tile([P, PAIRS * P], F32, name="shortfall")
         allowance = keep.tile([P, PAIRS, P], F32, name="allowance")
-        nc.vector.reciprocal(inverse[:, 0, :], floors[:, 1, 0, :])
         for a in range(TILES):
-            nc.scalar.activation(logs[:, 2 * a, :], p_mixed[a][:], ACT.Ln)
-            nc.scalar.activation(logs[:, 2 * a + 1, :], q_mixed[a][:], ACT.Ln)
-            nc.vector.scalar_tensor_tensor(cross[a][:], q_mixed[a][:], -FLOOR, logs[:, 2 * a, :], ALU.mult, ALU.mult)
-            nc.vector.scalar_tensor_tensor(own[a][:], q_mixed[a][:], FLOOR, logs[:, 2 * a + 1, :], ALU.mult, ALU.mult)
+            for b in {0: (0, 1), 1: (), 2: (2,), 3: (3,)}[a]:
+                nc.scalar.activation(p_logs[b], p_mixed[b][:], ACT.Ln)
+            pieces = halves if a == TILES - 1 else [slice(0, V)]
+            for cols in pieces:
+                nc.scalar.activation(q_logs[a][:, cols], q_mixed[a][:, cols], ACT.Ln)
+            for cols in pieces:
+                (nc.gpsimd if a in [] else nc.vector).tensor_tensor(gaps[a][:, cols], q_logs[a][:, cols], p_logs[a][:, cols], ALU.subtract)
+            for cols in pieces:
+                nc.vector.scalar_tensor_tensor(own[a][:, cols], q_mixed[a][:, cols], FLOOR, gaps[a][:, cols], ALU.mult, ALU.mult)
             if a == 1:
-                nc.scalar.activation(log_floors, floors_t[:].rearrange("p s a t -> p (s a t)"), ACT.Ln)
+                nc.scalar.activation(log_floors, floors[:].rearrange("p s a t -> p (s a t)"), ACT.Ln)
+                lowered = keep.tile([P, PAIRS * P], F32, name="lowered")
                 nc.gpsimd.tensor_tensor(margin[:], log_floors[:, : PAIRS * P], log_floors[:, PAIRS * P :], ALU.subtract)
-                nc.gpsimd.tensor_scalar(shortfall[:], margin[:], 1.0, -FREE, ALU.mult, ALU.add)
+                nc.gpsimd.tensor_scalar(lowered[:], margin[:], 1.0, -FREE, ALU.mult, ALU.add)
                 nc.gpsimd.tensor_tensor(
-                    allowance[:].rearrange("p a t -> p (a t)"), shortfall[:], floors_t[:, 1, :, :].rearrange("p a t -> p (a t)"), ALU.mult
+                    allowance[:].rearrange("p a t -> p (a t)"), lowered[:], floors[:, 1, :, :].rearrange("p a t -> p (a t)"), ALU.mult
                 )
+        inverse = keep.tile([P, PAIRS, P], F32, name="inverse", tag="gap1")
+        nc.scalar.activation(inverse[:].rearrange("p a t -> p (a t)"), log_floors[:, PAIRS * P :], ACT.Exp, scale=-1.0)
 
-        nc.vector.reciprocal(inverse[:, 1, :], floors[:, 1, 1, :])
         result = keep.tile([P, TILES, G], F32, name="result")
+        excess = keep.tile([P, PAIRS, P], F32, name="excess")
         for pair in range(PAIRS):
             total = bank(2 * pair, "total%d" % pair)
-            terms = [term[a][:, j * P : (j + 1) * P] for a in (2 * pair, 2 * pair + 1) for term in (cross, own) for j in range(HALF)]
-            terms = terms[:-HALF] + [allowance[:, pair, :]] + terms[-HALF:] if pair else terms + [allowance[:, pair, :]]
+            terms = [own[a][:, j * P : (j + 1) * P] for a in (2 * pair, 2 * pair + 1) for j in range(HALF)]
             for n, term in enumerate(terms):
                 add_transposed(total[:, 0:P], term, n == 0, n == len(terms) - 1)
+            nc.vector.tensor_tensor(excess[:, pair, :], total[:, 0:P], allowance[:, pair, :], ALU.add)
             nc.vector.scalar_tensor_tensor(
-                result[:, 2 * pair : 2 * pair + 2, :].rearrange("p t g -> p (t g)"), total[:, 0:P], 0.0, inverse[:, pair, :],
+                result[:, 2 * pair : 2 * pair + 2, :].rearrange("p t g -> p (t g)"), excess[:, pair, :], 0.0, inverse[:, pair, :],
                 ALU.max, ALU.mult,
             )
             nc.sync.dma_start(

@@ -46,12 +46,12 @@ def tile_picked_ydream_free_p_kernel(
             return tile
 
         def load_words(source, name):
-            tile = keep.tile([P, source.shape[2]], I32, name=name, align_bytes=64)
+            tile = keep.tile([P, source.shape[2]], I32, name=name, tag=name, align_bytes=64)
             nc.sync.dma_start(tile[:], source[0].rearrange("p c r -> p (c r)").bitcast(I32))
             return tile
 
         def load_scales(queue, source, name):
-            tile = keep.tile([P, source.shape[2]], U8, name=name, align_bytes=64)
+            tile = keep.tile([P, source.shape[2]], U8, name=name, tag=name, align_bytes=64)
             nc.gpsimd.memset(tile[:].bitcast(I32), 0)
             for q in range(4):
                 queue.dma_start(tile[32 * q : 32 * q + 4, :].bitcast(I32), source[0, 4 * q : 4 * q + 4, :].bitcast(I32))
@@ -63,7 +63,7 @@ def tile_picked_ydream_free_p_kernel(
             return tile
 
         def cast_views(raw, name):
-            grouped = keep.tile([P, raw.shape[2], PACK], BF16, name=name, align_bytes=64)
+            grouped = keep.tile([P, raw.shape[2], PACK], BF16, name=name, tag=name, align_bytes=64)
             dst = grouped[:].rearrange("p (c i) j -> p c j i", i=4)
             src = raw[:].rearrange("p j (c i) -> p c j i", i=4)
             return grouped, dst, src
@@ -71,42 +71,31 @@ def tile_picked_ydream_free_p_kernel(
         def quantise(grouped, codes, scales):
             nc.vector.quantize_mx(out=codes.bitcast(FP8X4), scales=scales, in_=grouped[:].rearrange("p c j -> p (c j)"))
 
-        def mx_tiles(name):
-            codes = keep.tile([P, 512], U32, name=name + "_codes", align_bytes=64)
+        def mx_tiles(name, tag):
+            codes = keep.tile([P, 512], U32, name=name + "_codes", tag=tag, align_bytes=64)
             scales = keep.tile([P, 512], U8, name=name + "_scales", align_bytes=64)
             return codes, scales
 
         halves = [slice(0, V // 2), slice(V // 2, V)]
         offs_sb = load_list(offs, "offs_sb")
         x_table = load_words(x_words, "x_table")
-        x_plane = load_scales(nc.scalar, x_scales, "x_plane")
-        obs_sb = load_list(obs, "obs_sb")
+        x_plane = load_scales(nc.sync, x_scales, "x_plane")
         wq_raw = load_weight(wq, slice(0, V), "wq_raw")
+        obs_sb = load_list(obs, "obs_sb")
         e_plane = load_scales(nc.sync, e_scales, "e_plane")
         wh_raw = load_weight(wh, slice(0, V), "wh_raw")
         wo_raw = load_weight(wo, slice(0, V), "wo_raw")
         e_table = load_words(e_words, "e_table")
 
-        x_codes, x_bytes = mx_tiles("x")
-        e_codes, e_bytes = mx_tiles("e")
-        wq_codes, wq_bytes = mx_tiles("wq")
-        wh_codes, wh_bytes = mx_tiles("wh")
-        wo_codes, wo_bytes = mx_tiles("wo")
-
-        def cast_on_gpsimd(raw, name):
-            grouped = keep.tile([P, raw.shape[2], PACK], BF16, name=name, tag=name, align_bytes=64)
-            nc.gpsimd.tensor_scalar(grouped[:], raw[:].rearrange("p j c -> p c j"), 1.0, 0.0, ALU.mult, ALU.add)
-            return grouped
+        x_codes, x_bytes = mx_tiles("x", "x_codes")
+        e_codes, e_bytes = mx_tiles("e", "e_codes")
+        wq_codes, wq_bytes = mx_tiles("wq", "wq_codes")
+        wh_codes, wh_bytes = mx_tiles("wh", "wh_codes")
 
         def cast_on_scalar(raw, name):
             grouped, dst, src = cast_views(raw, name)
             nc.scalar.copy(dst, src)
             return grouped
-
-        def gather_words(codes, table, offsets, h):
-            nc.vector.tensor_copy(
-                codes[:, h * 256 : (h + 1) * 256], table[:].bitcast(U32).indirect(offsets[:, h * 16 : (h + 1) * 16])
-            )
 
         ident = keep.tile([P, P], F32, name="ident")
         make_identity(nc, ident[:])
@@ -133,13 +122,11 @@ def tile_picked_ydream_free_p_kernel(
         def by_class(logits):
             return logits[:].rearrange("p (g d) -> p d g", d=D)
 
-        def peak(logits, name):
-            peaks = keep.tile([P, G], F32, name=name)
-            nc.vector.tensor_reduce(peaks[:], logits[:].rearrange("p (g d) -> p g d", d=D), AXIS.X, ALU.max)
-            return peaks
+        def peak(peaks, logits):
+            nc.vector.tensor_reduce(peaks, logits[:].rearrange("p (g d) -> p g d", d=D), AXIS.X, ALU.max)
 
         def shift(engine, shifted, source, peaks):
-            engine.tensor_tensor(shifted, source, peaks[:].unsqueeze(1).to_broadcast([P, D, G]), ALU.subtract)
+            engine.tensor_tensor(shifted, source, peaks.unsqueeze(1).to_broadcast([P, D, G]), ALU.subtract)
 
         def exponentials(powers, shifted):
             for t in range(2):
@@ -180,34 +167,32 @@ def tile_picked_ydream_free_p_kernel(
         p_floors_t = keep.tile([P, P], F32, name="p_floors_t", tag="p_floors_t", align_bytes=64)
 
         y = [bank(tile, "y%d" % tile) for tile in range(TILES)]
-        for tile in range(TILES):
+        for tile in (2, 3, 0, 1):
             product(y[tile], tile, x_codes, x_bytes, wq_codes, wq_bytes, True, True)
         z = [bank(TILES + tile, "z%d" % tile) for tile in range(TILES)]
 
         wh_grouped = cast_on_scalar(wh_raw, "wh_grouped")
-        wo_grouped = cast_on_gpsimd(wo_raw, "wo_grouped")
-        after_wh = keep.tile([P, 2, D, 2, G], F32, name="after_wh", tag="wh_raw", align_bytes=64)
-        after_wo = keep.tile([P, 2, D, G], F32, name="after_wo", tag="wo_raw", align_bytes=64)
-        p_powers = [after_wh[:, 0], keep.tile([P, D, 2, G], F32, name="p_powers1")[:]]
-        plain = after_wh[:, 1].rearrange("p d t g -> p (d t g)").rearrange("p (t d g) -> p t d g", t=2, d=D)
-        p_shifted = [keep.tile([P, D, G], F32, name="p_shifted0")[:], None, after_wo[:, 0], after_wo[:, 1]]
-        p_peaks = [peak(y[0], "p_peaks0"), peak(y[1], "p_peaks1")]
-        shift(nc.vector, p_shifted[0], by_class(y[0]), p_peaks[0])
-        p_peaks.append(peak(y[2], "p_peaks2"))
+        wo_grouped = cast_on_scalar(wo_raw, "wo_grouped")
+        both_powers = keep.tile([P, PAIRS, D, 2, G], F32, name="both_powers", tag="wo_raw", align_bytes=64)
+        p_powers = [both_powers[:, pair] for pair in range(PAIRS)]
+        p_shifted = [keep.tile([P, D, G], F32, name="p_shifted%d" % t)[:] if t != 1 else None for t in range(TILES)]
+        p_peaks = keep.tile([P, TILES, G], F32, name="p_peaks", tag="e_plane", align_bytes=64)
+        order = (2, 3, 0, 1)
+        for n, tile in enumerate(order):
+            peak(p_peaks[:, tile], y[tile])
+            if n > 0:
+                shift(nc.vector, p_shifted[order[n - 1]], by_class(y[order[n - 1]]), p_peaks[:, order[n - 1]])
         quantise(wh_grouped, wh_codes[:], wh_bytes[:])
         for tile in range(TILES):
             product(z[tile], tile, x_codes, x_bytes, wh_codes, wh_bytes, True, False)
-        p_peaks.append(peak(y[3], "p_peaks3"))
-        for t in range(2):
-            nc.scalar.copy(plain[:, t], by_class(y[2 + t]))
-            shift(nc.gpsimd, p_shifted[2 + t], plain[:, t], p_peaks[2 + t])
-        gather_words(e_codes, e_table, obs_sb, 0)
+        nc.vector.tensor_copy(e_codes[:], e_table[:].bitcast(U32).indirect(obs_sb[:]))
+        wo_codes, wo_bytes = mx_tiles("wo", "e_table")
         quantise(wo_grouped, wo_codes[:], wo_bytes[:])
-        gather_words(e_codes, e_table, obs_sb, 1)
         for tile in range(TILES):
             product(z[tile], tile, e_codes, e_bytes, wo_codes, wo_bytes, False, True)
-        p_shifted[1] = keep.tile([P, D, G], F32, name="p_shifted1", tag="wo_grouped", align_bytes=64)[:]
-        shift(nc.vector, p_shifted[1], by_class(y[1]), p_peaks[1])
+        after_wo = keep.tile([P, 2, V], F32, name="after_wo", tag="wo_grouped", align_bytes=64)
+        p_shifted[1] = after_wo[:, 0, :].rearrange("p (d g) -> p d g", d=D)
+        shift(nc.vector, p_shifted[1], by_class(y[1]), p_peaks[:, 1])
         exponentials(p_powers[1], p_shifted[2:])
         exponentials(p_powers[0], p_shifted[:2])
 
@@ -216,11 +201,11 @@ def tile_picked_ydream_free_p_kernel(
         p_mixed = mixtures(p_powers[0], p_sums, [0, 1], "p0", False, False, p_floors_t[:], floors[:, 0, 0, :])
 
         late = p_powers[1].rearrange("p d t g -> p d (t g)")
-        fold = keep.tile([P, HALF, P], F32, name="fold")
+        fold = after_wo[:, 1, :].rearrange("p (d c) -> p d c", d=HALF)
         fold2 = keep.tile([P, 2, P], F32, name="fold2")
         fold3 = keep.tile([P, P], F32, name="fold3")
         late_mixed = keep.tile([P, D, P], F32, name="late_mixed")
-        nc.gpsimd.tensor_tensor(fold[:], late[:, :HALF, :], late[:, HALF:, :], ALU.add)
+        nc.gpsimd.tensor_tensor(fold, late[:, :HALF, :], late[:, HALF:, :], ALU.add)
         nc.gpsimd.tensor_tensor(fold2[:], fold[:, :2, :], fold[:, 2:, :], ALU.add)
         nc.gpsimd.tensor_tensor(fold3[:], fold2[:, 0, :], fold2[:, 1, :], ALU.add)
         nc.gpsimd.tensor_scalar(floors[:, 0, 1, :], fold3[:], FLOOR / KEEP, 0.0, ALU.mult, ALU.add)
@@ -231,11 +216,12 @@ def tile_picked_ydream_free_p_kernel(
             )
         q_shifted = [keep.tile([P, D, G], F32, name="q_shifted%d" % t, tag="q_stage%d" % t)[:] for t in range(TILES)]
         q_powers = [keep.tile([P, D, 2, G], F32, name="q_powers%d" % pair)[:] for pair in range(PAIRS)]
-        q_peaks = [peak(z[0], "q_peaks0")]
+        q_peaks = keep.tile([P, TILES, G], F32, name="q_peaks")
+        peak(q_peaks[:, 0], z[0])
         for tile in range(TILES):
             if tile + 1 < TILES:
-                q_peaks.append(peak(z[tile + 1], "q_peaks%d" % (tile + 1)))
-            shift(nc.vector, q_shifted[tile], by_class(z[tile]), q_peaks[tile])
+                peak(q_peaks[:, tile + 1], z[tile + 1])
+            shift(nc.vector, q_shifted[tile], by_class(z[tile]), q_peaks[:, tile])
         for pair in range(PAIRS):
             exponentials(q_powers[pair], q_shifted[2 * pair : 2 * pair + 2])
         q_mixed = []
@@ -272,6 +258,12 @@ def tile_picked_ydream_free_p_kernel(
         for a in range(TILES):
             for b in {0: (0, 1), 1: (), 2: (2,), 3: (3,)}[a]:
                 nc.scalar.activation(p_logs[b], p_mixed[b][:], ACT.Ln)
+            if a == 0:
+                nc.scalar.activation(log_floors, floors[:].rearrange("p s a t -> p (s a t)"), ACT.Ln)
+                nc.vector.scalar_tensor_tensor(margin[:], log_floors[:, : PAIRS * P], -FREE, log_floors[:, PAIRS * P :], ALU.add, ALU.subtract)
+                nc.vector.tensor_tensor(
+                    allowance[:].rearrange("p a t -> p (a t)"), margin[:], floors[:, 1, :, :].rearrange("p a t -> p (a t)"), ALU.mult
+                )
             pieces = halves if a == TILES - 1 else [slice(0, V)]
             for cols in pieces:
                 nc.scalar.activation(q_logs[a][:, cols], q_mixed[a][:, cols], ACT.Ln)
@@ -279,14 +271,6 @@ def tile_picked_ydream_free_p_kernel(
                 (nc.gpsimd if a in [] else nc.vector).tensor_tensor(gaps[a][:, cols], q_logs[a][:, cols], p_logs[a][:, cols], ALU.subtract)
             for cols in pieces:
                 nc.vector.scalar_tensor_tensor(own[a][:, cols], q_mixed[a][:, cols], FLOOR, gaps[a][:, cols], ALU.mult, ALU.mult)
-            if a == 1:
-                nc.scalar.activation(log_floors, floors[:].rearrange("p s a t -> p (s a t)"), ACT.Ln)
-                lowered = keep.tile([P, PAIRS * P], F32, name="lowered")
-                nc.gpsimd.tensor_tensor(margin[:], log_floors[:, : PAIRS * P], log_floors[:, PAIRS * P :], ALU.subtract)
-                nc.gpsimd.tensor_scalar(lowered[:], margin[:], 1.0, -FREE, ALU.mult, ALU.add)
-                nc.gpsimd.tensor_tensor(
-                    allowance[:].rearrange("p a t -> p (a t)"), lowered[:], floors[:, 1, :, :].rearrange("p a t -> p (a t)"), ALU.mult
-                )
         inverse = keep.tile([P, PAIRS, P], F32, name="inverse", tag="gap1")
         nc.scalar.activation(inverse[:].rearrange("p a t -> p (a t)"), log_floors[:, PAIRS * P :], ACT.Exp, scale=-1.0)
 

@@ -171,7 +171,8 @@ def tile_picked_ydream_free_p_kernel(
             product(y[tile], tile, x_codes, x_bytes, wq_codes, wq_bytes, True, True)
         z = [bank(TILES + tile, "z%d" % tile) for tile in range(TILES)]
 
-        wh_grouped = cast_on_scalar(wh_raw, "wh_grouped")
+        wh_grouped = keep.tile([P, V, PACK], BF16, name="wh_grouped", tag="wh_grouped", align_bytes=64)
+        nc.gpsimd.tensor_scalar(wh_grouped[:], wh_raw[:].rearrange("p j c -> p c j"), 1.0, 0.0, ALU.mult, ALU.add)
         wo_grouped = cast_on_scalar(wo_raw, "wo_grouped")
         both_powers = keep.tile([P, PAIRS, D, 2, G], F32, name="both_powers", tag="wo_raw", align_bytes=64)
         p_powers = [both_powers[:, pair] for pair in range(PAIRS)]
@@ -235,12 +236,22 @@ def tile_picked_ydream_free_p_kernel(
             nc.vector.tensor_scalar(floors[:, 1, pair, :], summed[:], FLOOR / KEEP, None, ALU.mult)
             for a in range(2):
                 mixed = bank(TILES + 2 * pair + a, "q%d_mixed%d" % (pair, a))
-                for j in range(HALF):
-                    add_transposed(mixed[:, j * P : (j + 1) * P], powers[:, a * HALF + j, :, :].rearrange("p t g -> p (t g)"), j == 0, False)
                 q_mixed.append(mixed)
+                if 2 * pair + a < 2:
+                    for j in range(HALF):
+                        add_transposed(mixed[:, j * P : (j + 1) * P], powers[:, a * HALF + j, :, :].rearrange("p t g -> p (t g)"), j == 0, False)
         for a in range(TILES):
-            for j in range(HALF):
-                add_transposed(q_mixed[a][:, j * P : (j + 1) * P], floors[:, 1, a // 2, :], False, j == HALF - 1)
+            if a < 2:
+                for j in range(HALF):
+                    add_transposed(q_mixed[a][:, j * P : (j + 1) * P], floors[:, 1, a // 2, :], False, j == HALF - 1)
+            else:
+                added = keep.tile([P, HALF, P], F32, name="added%d" % a, tag="added%d" % a)
+                nc.vector.tensor_tensor(
+                    added[:], q_powers[1][:, (a % 2) * HALF : (a % 2 + 1) * HALF].rearrange("p d t g -> p d (t g)"),
+                    floors[:, 1, 1, :].unsqueeze(1).to_broadcast([P, HALF, P]), ALU.add,
+                )
+                for j in range(HALF):
+                    nc.tensor.transpose(q_mixed[a][:, j * P : (j + 1) * P], added[:, j, :], ident[:])
             if a == 1:
                 for b in range(2):
                     mixed = bank(2 + b, "p1_mixed%d" % b)
@@ -251,6 +262,7 @@ def tile_picked_ydream_free_p_kernel(
         log_floors = logs[:, 2 * TILES, :]
         p_logs = [logs[:, 2 * a, :] for a in range(TILES)]
         q_logs = [logs[:, 2 * a + 1, :] for a in range(TILES)]
+        p_logs[3] = keep.tile([P, V], F32, name="last_logs", tag="added2")[:]
         gaps = [keep.tile([P, V], F32, name="gap%d" % a, tag="gap%d" % a) for a in range(TILES)]
         own = [keep.tile([P, V], F32, name="own%d" % a) for a in range(TILES)]
         margin = keep.tile([P, PAIRS * P], F32, name="margin")

from contextlib import ExitStack

import concourse.mybir as mybir
from concourse.masks import make_identity

F32 = mybir.dt.float32
BF16 = mybir.dt.bfloat16
I32 = mybir.dt.int32
U32 = mybir.dt.uint32
U16 = mybir.dt.uint16
U8 = mybir.dt.uint8
FP8X4 = mybir.dt.float8_e4m3fn_x4
ALU = mybir.AluOpType
ACT = mybir.ActivationFunctionType
AXIS = mybir.AxisListType

P = 128
S = 512
V = 512
D = 8
G = V // D
PACK = 4
TILES = S // P
PAIRS = TILES // 2
HALF = D // 2
KEEP = 0.99
FLOOR = 0.00125
FREE = 0.3
FLOPS = 3 * 2 * 512 * S * V


def tile_picked_ydream_free_p_kernel(
    tc, x_words, x_scales, e_words, e_scales, wq, wh, wo, offs, obs, out
):
    nc = tc.nc
    with ExitStack() as ctx:
        keep = ctx.enter_context(tc.tile_pool(name="keep", bufs=1))
        psum = ctx.enter_context(tc.psum_pool(name="psum", bufs=1))

        def bank(index, name):
            return psum.tile([P, 512], F32, name=name, tag="bank%d" % index)

        def load_list(source, name):
            tile = keep.tile([P, S // 16], U16, name=name)
            nc.sync.dma_start(tile[:], source)
            return tile

        def load_words(source, name):
            tile = keep.tile([P, source.shape[2]], I32, name=name, tag=name, align_bytes=64)
            nc.sync.dma_start(tile[:], source[0].rearrange("p c r -> p (c r)").bitcast(I32))
            return tile

        def load_scales(queue, source, name):
            tile = keep.tile([P, source.shape[2]], U8, name=name, tag=name, align_bytes=64)
            nc.gpsimd.memset(tile[:].bitcast(I32), 0)
            for q in range(4):
                queue.dma_start(tile[32 * q : 32 * q + 4, :].bitcast(I32), source[0, 4 * q : 4 * q + 4, :].bitcast(I32))
            return tile

        def load_weight(source, cols, name):
            tile = keep.tile([P, PACK, cols.stop - cols.start], F32, name=name, tag=name, align_bytes=64)
            nc.sync.dma_start(tile[:], source.rearrange("(p j) c -> p j c", j=PACK)[:, :, cols])
            return tile

        def cast_views(raw, name):
            grouped = keep.tile([P, raw.shape[2], PACK], BF16, name=name, tag=name, align_bytes=64)
            dst = grouped[:].rearrange("p (c i) j -> p c j i", i=4)
            src = raw[:].rearrange("p j (c i) -> p c j i", i=4)
            return grouped, dst, src

        def quantise(grouped, codes, scales):
            nc.vector.quantize_mx(out=codes.bitcast(FP8X4), scales=scales, in_=grouped[:].rearrange("p c j -> p (c j)"))

        def mx_tiles(name, tag):
            codes = keep.tile([P, 512], U32, name=name + "_codes", tag=tag, align_bytes=64)
            scales = keep.tile([P, 512], U8, name=name + "_scales", align_bytes=64)
            return codes, scales

        halves = [slice(0, V // 2), slice(V // 2, V)]
        offs_sb = load_list(offs, "offs_sb")
        x_table = load_words(x_words, "x_table")
        x_plane = load_scales(nc.sync, x_scales, "x_plane")
        wq_raw = load_weight(wq, slice(0, V), "wq_raw")
        obs_sb = load_list(obs, "obs_sb")
        e_plane = load_scales(nc.sync, e_scales, "e_plane")
        wh_raw = load_weight(wh, slice(0, V), "wh_raw")
        wo_raw = load_weight(wo, slice(0, V), "wo_raw")
        e_table = load_words(e_words, "e_table")

        x_codes, x_bytes = mx_tiles("x", "x_codes")
        e_codes, e_bytes = mx_tiles("e", "e_codes")
        wq_codes, wq_bytes = mx_tiles("wq", "wq_codes")
        wh_codes, wh_bytes = mx_tiles("wh", "wh_codes")

        def cast_on_scalar(raw, name):
            grouped, dst, src = cast_views(raw, name)
            nc.scalar.copy(dst, src)
            return grouped

        ident = keep.tile([P, P], F32, name="ident")
        make_identity(nc, ident[:])
        wq_high = cast_on_scalar(wq_raw[:, :, halves[1]], "wq_high")

        nc.vector.tensor_copy(x_codes[:], x_table[:].bitcast(U32).indirect(offs_sb[:]))
        nc.vector.tensor_copy(x_bytes[:], x_plane[:].indirect(offs_sb[:]))
        wq_low, dst, src = cast_views(wq_raw[:, :, halves[0]], "wq_low")
        nc.vector.tensor_copy(dst, src)
        quantise(wq_low, wq_codes[:, halves[0]], wq_bytes[:, halves[0]])
        quantise(wq_high, wq_codes[:, halves[1]], wq_bytes[:, halves[1]])
        nc.vector.tensor_copy(e_bytes[:], e_plane[:].indirect(obs_sb[:]))

        def product(logits, tile, codes, scales, w_codes, w_scales, start, stop):
            rows = slice(tile * P, (tile + 1) * P)
            nc.tensor.matmul_mx(
                out=logits[:], lhsT=codes[:, rows].bitcast(FP8X4), lhsT_scale=scales[:, rows],
                rhs=w_codes[:].bitcast(FP8X4), rhs_scale=w_scales[:], start=start, stop=stop,
            )

        def add_transposed(dst, src, start, stop):
            nc.tensor.matmul(dst, src, ident[:], start=start, stop=stop, is_transpose=True)

        def by_class(logits):
            return logits[:].rearrange("p (g d) -> p d g", d=D)

        def peak(peaks, logits):
            nc.vector.tensor_reduce(peaks, logits[:].rearrange("p (g d) -> p g d", d=D), AXIS.X, ALU.max)

        def shift(engine, shifted, source, peaks):
            engine.tensor_tensor(shifted, source, peaks.unsqueeze(1).to_broadcast([P, D, G]), ALU.subtract)

        def exponentials(powers, shifted):
            for t in range(2):
                nc.scalar.activation(powers[:, :, t, :], shifted[t], ACT.Exp)

        def mixtures(powers, sums, banks, name, scale_on_vector, copy_on_vector, floors_t, floors):
            def block(d):
                return powers[:, d, :, :].rearrange("p t g -> p (t g)")

            def spread(a, mixed):
                for j in range(HALF):
                    add_transposed(mixed[:, j * P : (j + 1) * P], block(a * HALF + j), j == 0, False)

            def add_floors(mixed):
                for j in range(HALF):
                    add_transposed(mixed[:, j * P : (j + 1) * P], floors, False, j == HALF - 1)

            for d in range(D):
                add_transposed(sums[:, 0:P], block(d), d == 0, d == D - 1)
            first = bank(banks[0], name + "_mixed0")
            spread(0, first)
            if scale_on_vector:
                nc.vector.tensor_scalar(floors_t, sums[:, 0:P], FLOOR / KEEP, None, ALU.mult)
            else:
                nc.scalar.activation(floors_t, sums[:, 0:P], ACT.Copy, scale=FLOOR / KEEP)
            nc.tensor.transpose(sums[:, P : 2 * P], floors_t, ident[:])
            if copy_on_vector:
                nc.vector.tensor_copy(floors, sums[:, P : 2 * P])
            else:
                nc.scalar.copy(floors, sums[:, P : 2 * P])
            add_floors(first)
            second = bank(banks[1], name + "_mixed1")
            spread(1, second)
            add_floors(second)
            return [first, second]

        floors = keep.tile([P, 2, PAIRS, P], F32, name="floors")
        p_floors_t = keep.tile([P, P], F32, name="p_floors_t", tag="p_floors_t", align_bytes=64)

        y = [bank(tile, "y%d" % tile) for tile in range(TILES)]
        for tile in (2, 3, 0, 1):
            product(y[tile], tile, x_codes, x_bytes, wq_codes, wq_bytes, True, True)
        z = [bank(TILES + tile, "z%d" % tile) for tile in range(TILES)]

        wh_grouped = keep.tile([P, V, PACK], BF16, name="wh_grouped", tag="wh_grouped", align_bytes=64)
        nc.gpsimd.tensor_scalar(wh_grouped[:], wh_raw[:].rearrange("p j c -> p c j"), 1.0, 0.0, ALU.mult, ALU.add)
        wo_grouped = cast_on_scalar(wo_raw, "wo_grouped")
        both_powers = keep.tile([P, PAIRS, D, 2, G], F32, name="both_powers", tag="wo_raw", align_bytes=64)
        p_powers = [both_powers[:, pair] for pair in range(PAIRS)]
        p_shifted = [keep.tile([P, D, G], F32, name="p_shifted%d" % t)[:] if t != 1 else None for t in range(TILES)]
        p_peaks = keep.tile([P, TILES, G], F32, name="p_peaks", tag="e_plane", align_bytes=64)
        order = (2, 3, 0, 1)
        for n, tile in enumerate(order):
            peak(p_peaks[:, tile], y[tile])
            if n > 0:
                shift(nc.vector, p_shifted[order[n - 1]], by_class(y[order[n - 1]]), p_peaks[:, order[n - 1]])
        quantise(wh_grouped, wh_codes[:], wh_bytes[:])
        for tile in range(TILES):
            product(z[tile], tile, x_codes, x_bytes, wh_codes, wh_bytes, True, False)
        nc.vector.tensor_copy(e_codes[:], e_table[:].bitcast(U32).indirect(obs_sb[:]))
        wo_codes, wo_bytes = mx_tiles("wo", "e_table")
        quantise(wo_grouped, wo_codes[:], wo_bytes[:])
        for tile in range(TILES):
            product(z[tile], tile, e_codes, e_bytes, wo_codes, wo_bytes, False, True)
        after_wo = keep.tile([P, 2, V], F32, name="after_wo", tag="wo_grouped", align_bytes=64)
        p_shifted[1] = after_wo[:, 0, :].rearrange("p (d g) -> p d g", d=D)
        shift(nc.vector, p_shifted[1], by_class(y[1]), p_peaks[:, 1])
        exponentials(p_powers[1], p_shifted[2:])
        exponentials(p_powers[0], p_shifted[:2])

        p_sums = bank(TILES - 1, "p0_sums")
        p_floors = keep.tile([P, P], F32, name="p_floors", tag="p_floors", align_bytes=64)
        p_mixed = mixtures(p_powers[0], p_sums, [0, 1], "p0", False, False, p_floors_t[:], floors[:, 0, 0, :])

        late = p_powers[1].rearrange("p d t g -> p d (t g)")
        fold = after_wo[:, 1, :].rearrange("p (d c) -> p d c", d=HALF)
        fold2 = keep.tile([P, 2, P], F32, name="fold2")
        fold3 = keep.tile([P, P], F32, name="fold3")
        late_mixed = keep.tile([P, D, P], F32, name="late_mixed")
        nc.gpsimd.tensor_tensor(fold, late[:, :HALF, :], late[:, HALF:, :], ALU.add)
        nc.gpsimd.tensor_tensor(fold2[:], fold[:, :2, :], fold[:, 2:, :], ALU.add)
        nc.gpsimd.tensor_tensor(fold3[:], fold2[:, 0, :], fold2[:, 1, :], ALU.add)
        nc.gpsimd.tensor_scalar(floors[:, 0, 1, :], fold3[:], FLOOR / KEEP, 0.0, ALU.mult, ALU.add)
        for a in range(2):
            nc.gpsimd.tensor_tensor(
                late_mixed[:, a * HALF : (a + 1) * HALF, :], late[:, a * HALF : (a + 1) * HALF, :],
                floors[:, 0, 1, :].unsqueeze(1).to_broadcast([P, HALF, P]), ALU.add,
            )
        q_shifted = [keep.tile([P, D, G], F32, name="q_shifted%d" % t, tag="q_stage%d" % t)[:] for t in range(TILES)]
        q_powers = [keep.tile([P, D, 2, G], F32, name="q_powers%d" % pair)[:] for pair in range(PAIRS)]
        q_peaks = keep.tile([P, TILES, G], F32, name="q_peaks")
        peak(q_peaks[:, 0], z[0])
        for tile in range(TILES):
            if tile + 1 < TILES:
                peak(q_peaks[:, tile + 1], z[tile + 1])
            shift(nc.vector, q_shifted[tile], by_class(z[tile]), q_peaks[:, tile])
        for pair in range(PAIRS):
            exponentials(q_powers[pair], q_shifted[2 * pair : 2 * pair + 2])
        q_mixed = []
        for pair in range(PAIRS):
            powers = q_powers[pair]
            halved = keep.tile([P, HALF, 2, G], F32, name="halved%d" % pair)
            summed = keep.tile([P, P], F32, name="summed%d" % pair)
            for tiles in [slice(0, 2)] if pair == 0 else [slice(0, 1), slice(1, 2)]:
                nc.vector.tensor_tensor(halved[:, :, tiles, :], powers[:, :HALF, tiles, :], powers[:, HALF:, tiles, :], ALU.add)
            nc.vector.tensor_reduce(summed[:], halved[:].rearrange("p d t g -> p (t g) d"), AXIS.X, ALU.add)
            nc.vector.tensor_scalar(floors[:, 1, pair, :], summed[:], FLOOR / KEEP, None, ALU.mult)
            for a in range(2):
                mixed = bank(TILES + 2 * pair + a, "q%d_mixed%d" % (pair, a))
                q_mixed.append(mixed)
                if 2 * pair + a < 2:
                    for j in range(HALF):
                        add_transposed(mixed[:, j * P : (j + 1) * P], powers[:, a * HALF + j, :, :].rearrange("p t g -> p (t g)"), j == 0, False)
        for a in range(TILES):
            if a < 2:
                for j in range(HALF):
                    add_transposed(q_mixed[a][:, j * P : (j + 1) * P], floors[:, 1, a // 2, :], False, j == HALF - 1)
            else:
                added = keep.tile([P, HALF, P], F32, name="added%d" % a, tag="added%d" % a)
                nc.vector.tensor_tensor(
                    added[:], q_powers[1][:, (a % 2) * HALF : (a % 2 + 1) * HALF].rearrange("p d t g -> p d (t g)"),
                    floors[:, 1, 1, :].unsqueeze(1).to_broadcast([P, HALF, P]), ALU.add,
                )
                for j in range(HALF):
                    nc.tensor.transpose(q_mixed[a][:, j * P : (j + 1) * P], added[:, j, :], ident[:])
            if a == 1:
                for b in range(2):
                    mixed = bank(2 + b, "p1_mixed%d" % b)
                    for j in range(HALF):
                        nc.tensor.transpose(mixed[:, j * P : (j + 1) * P], late_mixed[:, b * HALF + j, :], ident[:])
                    p_mixed.append(mixed)
        logs = keep.tile([P, 2 * TILES + 1, V], F32, name="logs", tag="q_stage%d" % (TILES - 1))
        log_floors = logs[:, 2 * TILES, :]
        p_logs = [logs[:, 2 * a, :] for a in range(TILES)]
        q_logs = [logs[:, 2 * a + 1, :] for a in range(TILES)]
        p_logs[3] = keep.tile([P, V], F32, name="last_logs", tag="added2")[:]
        gaps = [keep.tile([P, V], F32, name="gap%d" % a, tag="gap%d" % a) for a in range(TILES)]
        own = [keep.tile([P, V], F32, name="own%d" % a) for a in range(TILES)]
        margin = keep.tile([P, PAIRS * P], F32, name="margin")
        allowance = keep.tile([P, PAIRS, P], F32, name="allowance")
        for a in range(TILES):
            for b in {0: (0, 1), 1: (), 2: (2,), 3: (3,)}[a]:
                nc.scalar.activation(p_logs[b], p_mixed[b][:], ACT.Ln)
            if a == 0:
                nc.scalar.activation(log_floors, floors[:].rearrange("p s a t -> p (s a t)"), ACT.Ln)
                nc.vector.scalar_tensor_tensor(margin[:], log_floors[:, : PAIRS * P], -FREE, log_floors[:, PAIRS * P :], ALU.add, ALU.subtract)
                nc.vector.tensor_tensor(
                    allowance[:].rearrange("p a t -> p (a t)"), margin[:], floors[:, 1, :, :].rearrange("p a t -> p (a t)"), ALU.mult
                )
            pieces = halves if a == TILES - 1 else [slice(0, V)]
            for cols in pieces:
                nc.scalar.activation(q_logs[a][:, cols], q_mixed[a][:, cols], ACT.Ln)
            for cols in pieces:
                (nc.gpsimd if a in [] else nc.vector).tensor_tensor(gaps[a][:, cols], q_logs[a][:, cols], p_logs[a][:, cols], ALU.subtract)
            for cols in pieces:
                nc.vector.scalar_tensor_tensor(own[a][:, cols], q_mixed[a][:, cols], FLOOR, gaps[a][:, cols], ALU.mult, ALU.mult)
        inverse = keep.tile([P, PAIRS, P], F32, name="inverse", tag="gap1")
        nc.scalar.activation(inverse[:].rearrange("p a t -> p (a t)"), log_floors[:, PAIRS * P :], ACT.Exp, scale=-1.0)

        result = keep.tile([P, TILES, G], F32, name="result")
        excess = keep.tile([P, PAIRS, P], F32, name="excess")
        for pair in range(PAIRS):
            total = bank(2 * pair, "total%d" % pair)
            terms = [own[a][:, j * P : (j + 1) * P] for a in (2 * pair, 2 * pair + 1) for j in range(HALF)]
            for n, term in enumerate(terms):
                add_transposed(total[:, 0:P], term, n == 0, n == len(terms) - 1)
            nc.vector.tensor_tensor(excess[:, pair, :], total[:, 0:P], allowance[:, pair, :], ALU.add)
            nc.vector.scalar_tensor_tensor(
                result[:, 2 * pair : 2 * pair + 2, :].rearrange("p t g -> p (t g)"), excess[:, pair, :], 0.0, inverse[:, pair, :],
                ALU.max, ALU.mult,
            )
            nc.sync.dma_start(
                out[2 * pair * P : (2 * pair + 2) * P, :].rearrange("(t p) g -> p t g", p=P), result[:, 2 * pair : 2 * pair + 2, :]
            )
